import numpy as np, ml_dtypes
CORES = [1,3,5,9,11,13]
N = 6
import mx_ref
NC, G, MB = 128, 2, 3
C = np.float32(0.031)
BF = ml_dtypes.bfloat16
def cut(t, i, w=512):
    return t[:, w * i:w * i + w]
def tile(rs):
    return np.stack(rs, axis=2).reshape(128, -1).astype(BF)
def layer(w, X):
    out = []
    for i in range(G):
        for t in range(len(X)):
            p = mx_ref.matmul(mx_ref.quantize(cut(w, len(X) * i + t)), X[t])
            z = p if t == 0 else z + p
        out.append(z)
    return out
def act(Z):
    return [np.maximum(s * z, 0) * C for z in Z for s in (1, -1)]
def setup_inputs(rng):
    def f(*shape):
        return mx_ref.flush((rng.standard_normal(shape, dtype=np.float32) * np.exp2(rng.integers(-2, 3, shape[:-1] + (1,)))).astype(BF))
    return {"x": f(N, 128, 4 * NC), "w1": f(N, 128, G * 512), "w2": f(N, 128, 512), "px": f(N, 128, MB * 4 * NC), "pw": f(N, 128, G * 512)}
def setup_inputs_blocks(rng):
    d = setup_inputs(rng)
    for k in ("x", "w1", "w2", "px"): d[k] = mx_ref.spread(d[k], rng, 4)
    for k in ("pw",): d[k] = mx_ref.spread(d[k], rng, 1)
    return d
def setup_inputs_wide(rng):
    d = setup_inputs(rng)
    for k in ("x", "w1", "w2", "px"): d[k] = mx_ref.flush((d[k].astype(np.float32) * np.exp2(rng.integers(-6, 7, (N, 1, 1))).astype(np.float32)).astype(BF))
    return d
def setup_inputs_zeros(rng):
    d = setup_inputs(rng); v = d["x"].reshape(N, 128, -1, 4).copy()
    v[np.broadcast_to((rng.random((N, 1, v.shape[2], 1)) < 0.33), v.shape)] = 0
    d["x"] = v.reshape(d["x"].shape)
    return d
def reference(x, w1, w2, px, pw):
    H = [mx_ref.quantize(tile(act(layer(w1[j], [mx_ref.quantize(x[j])])))) for j in range(N)]
    y = np.zeros((N, 128, N * NC), np.float32)
    for r in range(N):
        qw = mx_ref.quantize(w2[r])
        for j in range(N):
            y[r][:, NC * j:NC * j + NC] = mx_ref.matmul(qw, H[j])
    z = np.full((N, 128, MB * G * NC), np.nan, np.float32)
    for m in range(MB):
        a = mx_ref.quantize(cut(px[N - 1], m, 4 * NC))
        for s in range(N - 1):
            a = mx_ref.quantize(tile(act(layer(pw[s], [a]))))
        Z = layer(pw[N - 1], [a])
        for i in range(G):
            z[N - 1][:, NC * (G * m + i):NC * (G * m + i) + NC] = Z[i]
    return {"y": y, "z": z}

@@ -1,0 +1,274 @@
+from concourse.bass import DstId, RemoteDMATransfer
+from concourse.mybir import dt, AluOpType, ActivationFunctionType
+
+NC = 128
+G = 2
+MB = 3
+SIM = 16
+C = 0.031
+
+HOST = [[0, 1, 1, 3, 4, 5],
+        [0, 2, 1, 4, 4, 5],
+        [0, 2, 2, 3, 3, 5]]
+ORDER = [["h", (0, 0), (1, 0), (2, 0), "near", "far"],
+         ["h", (0, 1), (0, 2), "near", (1, 2), "far"],
+         ["h", (1, 1), (2, 1), (2, 2), "near", "far"],
+         ["h", "near", (0, 3), "far", (2, 3), (2, 4)],
+         ["h", "near", "far", (0, 4), (1, 3), (1, 4)],
+         ["h", "near", "far", (2, 5), (0, 5), (1, 5)]]
+LEAVE = {0: [[(0,)], [(1, 2)]]}
+
+BF, CODE, U8, F32 = "bfloat16", "float8_e4m3fn_x4", "uint8", "float32"
+SCRATCH = {
+    "xb": ("sbuf", [128, 512], BF), "w1b": ("sbuf", [128, 1024], BF), "w2b": ("sbuf", [128, 512], BF),
+    "pwb": ("sbuf", [128, 1024], BF), "pxb": ("sbuf", [128, 1536], BF),
+    "ht": ("sbuf", [128, 512], BF), "ct": ("sbuf", [128, 1536], BF),
+    "yb": ("sbuf", [128, 768], F32), "zb": ("sbuf", [128, 768], F32),
+    "ps": ("psum", [128, 4096], F32),
+}
+for _n, _w in [("x", 128), ("w1", 256), ("w2", 128), ("pw", 256), ("pr", 256), ("h", 768)] + [("a%d" % k, 384) for k in range(6)]:
+    SCRATCH[_n + "q"] = ("sbuf", [128, _w], CODE)
+    SCRATCH[_n + "s"] = ("sbuf", [128, _w], U8)
+SEMAPHORES = (["ld_x", "ld_w1", "ld_w2", "ld_pw", "ld_px0", "ld_px1", "q_xw", "q_pw", "q_w2", "q_px",
+               "mm_h0", "mm_h1", "ac_h", "ve_h", "q_h", "mm_near", "mm_far", "cp_near", "cp_far", "st"]
+              + ["%s_%d" % (n, k) for k in range(3) for n in ("mm0", "mm1", "ac", "ve", "q")]
+              + ["nc", "np", "far", "pwin", "a0", "in0", "in1", "in2", "rc", "rp", "tc", "tp", "sent"])
+
+
+def bits(mask):
+    return [1 << b for b in range(16) if mask >> b & 1]
+
+
+def share(mask, k, i):
+    b = bits(mask)
+    n = len(b) // k
+    return sum(b[n * i:n * i + n])
+
+
+def plan(T, topo):
+    cores = T.cores
+    n = len(cores)
+    calls = {c: [] for c in range(SIM)}
+    need = {c: {} for c in range(SIM)}
+
+    def near(c):
+        return [d for d in cores if d != c and topo.chip(d) == topo.chip(c)]
+
+    def far(c):
+        return [d for d in cores if topo.chip(d) != topo.chip(c)]
+
+    def helpers(c, die):
+        return [k for k in range(SIM) if k not in cores and topo.chip(k) == topo.chip(c) and topo.die(k) == die
+                and topo.may_write(k, far(c)[0])]
+
+    def put(src, waits, moves):
+        for part in range(2):
+            calls[src].append((waits[part], part, moves))
+            for buf, lo, hi, dsts, mask, sems in moves:
+                for d in dsts:
+                    need[d][sems[part]] = need[d].get(sems[part], 0) + len(bits(mask))
+
+    on = {c: topo.mask(c, [d for d in range(SIM) if d != c and topo.chip(d) == topo.chip(c)][0]) for c in range(SIM)}
+    off = {c: topo.mask(c, [d for d in range(SIM) if topo.chip(d) != topo.chip(c)][0]) for c in range(SIM)}
+    last, first = cores[n - 1], cores[0]
+
+    hw = MB * NC // 2
+    ports = [helpers(last, topo.die(last))[0], helpers(last, 1 - topo.die(last))[0]]
+    put(last, [[("q_px", 2)]] * 2, [("a0", hw * i, hw * i + hw, [p], share(on[last], 2, i), ("rc", "rp")) for i, p in enumerate(ports)])
+    for i, p in enumerate(ports):
+        put(p, [[("rc", None)], [("rp", None)]], [("a0", hw * i, hw * i + hw, [first], off[p], ("a0", "a0"))])
+
+    used = set()
+    for j, c in enumerate(cores):
+        lo, hi = NC * j, NC * j + NC
+        if topo.may_write(c, far(c)[0]) and topo.chip(c) == topo.chip(first):
+            put(c, [[("q_h", 1)]] * 2, [("h", lo, hi, near(c), on[c] & ~off[c], ("nc", "np")), ("h", lo, hi, far(c), off[c], ("far", "far"))])
+        else:
+            p = [k for k in helpers(c, topo.die(c)) + helpers(c, 1 - topo.die(c)) if k not in used][0]
+            used.add(p)
+            put(c, [[("q_h", 1)]] * 2, [("h", lo, hi, near(c) + [p], on[c], ("nc", "np"))])
+            put(p, [[("nc", None)], [("np", None)]], [("h", lo, hi, far(c), off[p], ("far", "far"))])
+
+    for j, c in enumerate(cores):
+        to = sorted({HOST[m][j] for m in range(MB)} - {j})
+        if to:
+            put(c, [[("q_pw", 1)]] * 2, [("pw", 0, G * NC, [cores[k] for k in to], on[c], ("pwin", "pwin"))])
+
+    sem_of = {}
+    for j, c in enumerate(cores):
+        jobs = [w for w in ORDER[j] if isinstance(w, tuple)]
+        slot = {w: k for k, w in enumerate(jobs)}
+        leave = [(m, s) for m, s in jobs if s < n - 1 and HOST[m][s + 1] != j]
+        for group in LEAVE.get(j, [[(m,)] for m, s in leave]):
+            waits, moves = [], []
+            for i, run in enumerate(group):
+                outs = [v for m in run for v in leave if v[0] == m]
+                waits += [("q_%d" % slot[v], 1) for v in outs]
+                to = HOST[run[0]][outs[0][1] + 1]
+                d, buf, sem = cores[to], "a%d" % (outs[0][1] + 1), "in%d" % run[0]
+                lo, hi = NC * run[0], NC * run[-1] + NC
+                parts = {1: 1, 2: 2}.get(len(group), 4)
+                for m in run:
+                    sem_of[to, m] = sem
+                if topo.may_write(c, d):
+                    mask = on[c] if topo.chip(c) == topo.chip(d) else off[c]
+                    moves.append((buf, lo, hi, [d], share(mask, parts, i), (sem, sem)))
+                else:
+                    p = helpers(c, topo.die(c))[0]
+                    moves.append((buf, lo, hi, [p], share(on[c], parts, i), ("tc", "tp")))
+                    put(p, [[("tc", None)], [("tp", None)]], [(buf, lo, hi, [d], off[p], (sem, sem))])
+            put(c, [waits, waits], moves)
+    return calls, need, sem_of
+
+
+def half(buf, part):
+    return buf + ("q" if part == 0 else "s")
+
+
+def rank_program(g, core, T, topo):
+    calls, need, sem_of = plan(T, topo)
+    rank = T.rank_of(core)
+    if rank is not None:
+        compute(g, rank, T, topo, need[core], sem_of)
+    sent = 0
+    for waits, part, moves in calls[core]:
+        for name, val in waits:
+            g.wait_ge(T.sem[name], need[core][name] if val is None else val)
+        trs = []
+        for buf, lo, hi, dsts, mask, sems in moves:
+            ap = T[half(buf, part)][:, lo:hi]
+            out = T[half("pr" if buf == "pw" else buf, part)][:, lo:hi]
+            if part == 0:
+                ap, out = ap.bitcast(dt.uint8), out.bitcast(dt.uint8)
+            trs.append((ap, out, dsts, mask, T.sem[sems[part]]))
+            sent += len(bits(mask))
+        if len(trs) == 1 and len(trs[0][2]) == 1:
+            ap, out, dsts, mask, sem = trs[0]
+            rid, pid, _ = topo.addr(dsts[0])
+            g.remote_dma(out, ap, sem, T.sem.sent, pid, rid, mask)
+        else:
+            g.remote_dma_fused([RemoteDMATransfer(
+                dst_ids=[DstId(rid=topo.addr(d)[0], pnc=topo.addr(d)[1]) for d in dsts],
+                dma_engine_mask=mask, remote_sem=sem, srcs=[ap], dsts=[out for d in dsts], alu_op=0)
+                for ap, out, dsts, mask, sem in trs], local_sem=T.sem.sent)
+    if sent:
+        g.wait_ge(T.sem.sent, sent)
+
+
+def compute(g, rank, T, topo, need, sem_of):
+    n = len(T.cores)
+    S = T.sem
+    last = rank == n - 1
+    te, ve, ac, sy = g.tensor, g.vector, g.scalar, g.sync
+    Relu, Copy = ActivationFunctionType.Relu, ActivationFunctionType.Copy
+    mult, mx = AluOpType.mult, AluOpType.max
+    seen = set()
+
+    def wait(q, qn, name, val=None):
+        v = need[name] if val is None else val
+        if (qn, name, v) not in seen:
+            seen.add((qn, name, v))
+            q.wait_ge(S[name], v)
+
+    hw = 4 * MB * NC // 2
+    if last:
+        sy.dma_start(T.pxb[:, 0:hw], T.px[:, 0:hw]).then_inc(S.ld_px0, 16)
+        ac.dma_start(T.pxb[:, hw:2 * hw], T.px[:, hw:2 * hw]).then_inc(S.ld_px1, 16)
+    sy.dma_start(T.xb[:], T.x[:]).then_inc(S.ld_x, 16)
+    ac.dma_start(T.w1b[:], T.w1[:]).then_inc(S.ld_w1, 16)
+    sy.dma_start(T.pwb[:], T.pw[:]).then_inc(S.ld_pw, 16)
+    ac.dma_start(T.w2b[:], T.w2[:]).then_inc(S.ld_w2, 16)
+
+    if last:
+        for i in range(2):
+            wait(ve, "v", "ld_px%d" % i, 16)
+            lo, hi = hw // 4 * i, hw // 4 * (i + 1)
+            ve.quantize_mx(T.a0q[:, lo:hi], T.a0s[:, lo:hi], T.pxb[:, 4 * lo:4 * hi]).then_inc(S.q_px, 1)
+    wait(ve, "v", "ld_x", 16)
+    ve.quantize_mx(T.xq[:, 0:128], T.xs[:, 0:128], T.xb[:, 0:512]).then_inc(S.q_xw, 1)
+    wait(ve, "v", "ld_w1", 16)
+    ve.quantize_mx(T.w1q[:, 0:256], T.w1s[:, 0:256], T.w1b[:, 0:1024]).then_inc(S.q_xw, 1)
+
+    def late_inputs():
+        wait(ve, "v", "ld_pw", 16)
+        ve.quantize_mx(T.pwq[:, 0:256], T.pws[:, 0:256], T.pwb[:, 0:1024]).then_inc(S.q_pw, 1)
+        wait(ve, "v", "ld_w2", 16)
+        ve.quantize_mx(T.w2q[:, 0:128], T.w2s[:, 0:128], T.w2b[:, 0:512]).then_inc(S.q_w2, 1)
+
+    def tag_mm(tag, i):
+        return "mm_h%d" % i if tag == "h" else "mm%d_%s" % (i, tag)
+
+    def products(tag, bank, w, ws, q, s, lo):
+        for i in range(G):
+            te.matmul_mx(T.ps[:, 512 * (bank + i):512 * (bank + i) + NC], w[:, NC * i:NC * i + NC], ws[:, NC * i:NC * i + NC],
+                         q[:, lo:lo + NC], s[:, lo:lo + NC], True, True).then_inc(S[tag_mm(tag, i)], 1)
+
+    def tile(tag, bank, tb, at, q, s, lo, sem):
+        z0, z1 = T.ps[:, 512 * bank:512 * bank + NC], T.ps[:, 512 * bank + 512:512 * bank + 512 + NC]
+        a, v = S["ac_%s" % tag], S["ve_%s" % tag]
+        e = at + 4 * NC
+        wait(ac, "a", tag_mm(tag, 0), 1)
+        ac.activation(tb[:, at:e:4], z0, Relu, scale=C).then_inc(a, 1)
+        ac.activation(tb[:, at + 1:e:4], z0, Relu, scale=-C).then_inc(a, 1)
+        wait(ve, "v", tag_mm(tag, 1), 1)
+        ve.tensor_scalar(tb[:, at + 2:e:4], z1, C, 0.0, mult, mx).then_inc(v, 1)
+        ve.tensor_scalar(tb[:, at + 3:e:4], z1, -C, 0.0, mult, mx).then_inc(v, 1)
+        wait(ve, "v", "ve_%s" % tag, 2)
+        wait(ve, "v", "ac_%s" % tag, 2)
+        ve.quantize_mx(q[:, lo:lo + NC], s[:, lo:lo + NC], tb[:, at:e]).then_inc(S[sem], 1)
+
+    mine = [j for j in range(n) if topo.chip(T.cores[j]) == topo.chip(T.cores[rank])]
+    slot = 0
+    where = {}
+    stores = 0
+    for job in ORDER[rank]:
+        if job == "h":
+            wait(te, "t", "q_xw", 2)
+            products("h", 0, T.w1q, T.w1s, T.xq, T.xs, 0)
+            tile("h", 0, T.ht, 0, T.hq, T.hs, NC * rank, "q_h")
+            late_inputs()
+        elif job in ("near", "far"):
+            ranks = mine if job == "near" else [j for j in range(n) if j not in mine]
+            lo, hi = NC * ranks[0], NC * ranks[-1] + NC
+            bank = 0 if job == "near" else 1
+            wait(te, "t", "q_w2", 1)
+            wait(te, "t", "q_h", 1)
+            for name in (("nc", "np") if job == "near" else ("far",)):
+                wait(te, "t", name)
+            z = T.ps[:, 512 * bank:512 * bank + hi - lo]
+            te.matmul_mx(z, T.w2q[:, 0:NC], T.w2s[:, 0:NC], T.hq[:, lo:hi], T.hs[:, lo:hi], True, True).then_inc(S["mm_" + job], 1)
+            wait(ac, "a", "mm_" + job, 1)
+            ac.activation(T.yb[:, lo:hi], z, Copy).then_inc(S["cp_" + job], 1)
+            wait(sy, "s", "cp_" + job, 1)
+            sy.dma_start(T.y[:, lo:hi], T.yb[:, lo:hi]).then_inc(S.st, 16)
+            stores += 1
+        else:
+            m, s = job
+            bank = 2 + 2 * slot
+            tag = str(slot)
+            if s > 0 and HOST[m][s - 1] == rank:
+                wait(te, "t", "q_%d" % where[m], 1)
+            else:
+                wait(te, "t", sem_of[rank, m] if s else "a0")
+            if s == rank:
+                wait(te, "t", "q_pw", 1)
+                w, ws = T.pwq, T.pws
+            else:
+                wait(te, "t", "pwin")
+                w, ws = T.prq, T.prs
+            products(tag, bank, w, ws, T["a%dq" % s], T["a%ds" % s], NC * m)
+            if s < n - 1:
+                tile(tag, bank, T.ct, 512 * slot, T["a%dq" % (s + 1)], T["a%ds" % (s + 1)], NC * m, "q_%d" % slot)
+            else:
+                lo = G * NC * m
+                wait(ac, "a", "mm0_" + tag, 1)
+                ac.activation(T.zb[:, lo:lo + NC], T.ps[:, 512 * bank:512 * bank + NC], Copy).then_inc(S["ac_" + tag], 1)
+                wait(ve, "v", "mm1_" + tag, 1)
+                ve.tensor_copy(T.zb[:, lo + NC:lo + 2 * NC], T.ps[:, 512 * bank + 512:512 * bank + 512 + NC]).then_inc(S["ve_" + tag], 1)
+                wait(sy, "s", "ac_" + tag, 1)
+                wait(sy, "s", "ve_" + tag, 1)
+                sy.dma_start(T.z[:, lo:lo + 2 * NC], T.zb[:, lo:lo + 2 * NC]).then_inc(S.st, 16)
+                stores += 1
+            where[m] = slot
+            slot += 1
+    wait(sy, "s", "st", 16 * stores)

@@ -8,15 +8,14 @@ SIM = 16
 C = 0.031
 
 HOST = [[0, 1, 1, 3, 4, 5],
-        [0, 2, 1, 4, 4, 5],
-        [0, 2, 2, 3, 3, 5]]
+        [0, 2, 1, 3, 3, 5],
+        [0, 2, 2, 4, 4, 5]]
 ORDER = [["h", (0, 0), (1, 0), (2, 0), "near", "far"],
          ["h", (0, 1), (0, 2), "near", (1, 2), "far"],
          ["h", (1, 1), (2, 1), (2, 2), "near", "far"],
-         ["h", "near", (0, 3), "far", (2, 3), (2, 4)],
-         ["h", "near", "far", (0, 4), (1, 3), (1, 4)],
-         ["h", "near", "far", (2, 5), (0, 5), (1, 5)]]
-LEAVE = {0: [[(0,)], [(1, 2)]]}
+         ["h", "near", (0, 3), "far", (1, 3), (1, 4)],
+         ["h", "near", "far", (0, 4), (2, 3), (2, 4)],
+         ["h", "near", "far", (0, 5), (1, 5), (2, 5)]]
 
 BF, CODE, U8, F32 = "bfloat16", "float8_e4m3fn_x4", "uint8", "float32"
 SCRATCH = {
@@ -29,20 +28,15 @@ SCRATCH = {
 for _n, _w in [("x", 128), ("w1", 256), ("w2", 128), ("pw", 256), ("pr", 256), ("h", 768)] + [("a%d" % k, 384) for k in range(6)]:
     SCRATCH[_n + "q"] = ("sbuf", [128, _w], CODE)
     SCRATCH[_n + "s"] = ("sbuf", [128, _w], U8)
-SEMAPHORES = (["ld_x", "ld_w1", "ld_w2", "ld_pw", "ld_px0", "ld_px1", "q_xw", "q_pw", "q_w2", "q_px",
+SEMAPHORES = (["ld_x", "ld_w1", "ld_w2", "ld_pw", "q_xw", "q_pw", "q_w2",
                "mm_h0", "mm_h1", "ac_h", "ve_h", "q_h", "mm_near", "mm_far", "cp_near", "cp_far", "st"]
               + ["%s_%d" % (n, k) for k in range(3) for n in ("mm0", "mm1", "ac", "ve", "q")]
-              + ["nc", "np", "far", "pwin", "a0", "in0", "in1", "in2", "rc", "rp", "tc", "tp", "sent"])
+              + ["%s%d" % (n, m) for m in range(MB) for n in ("ld_px", "q_px", "rc", "rp", "in")]
+              + ["nc", "np", "far", "pwin", "tc", "tp", "sent"])
 
 
 def bits(mask):
     return [1 << b for b in range(16) if mask >> b & 1]
-
-
-def share(mask, k, i):
-    b = bits(mask)
-    n = len(b) // k
-    return sum(b[n * i:n * i + n])
 
 
 def plan(T, topo):
@@ -72,11 +66,12 @@ def plan(T, topo):
     off = {c: topo.mask(c, [d for d in range(SIM) if topo.chip(d) != topo.chip(c)][0]) for c in range(SIM)}
     last, first = cores[n - 1], cores[0]
 
-    hw = MB * NC // 2
     ports = [helpers(last, topo.die(last))[0], helpers(last, 1 - topo.die(last))[0]]
-    put(last, [[("q_px", 2)]] * 2, [("a0", hw * i, hw * i + hw, [p], share(on[last], 2, i), ("rc", "rp")) for i, p in enumerate(ports)])
-    for i, p in enumerate(ports):
-        put(p, [[("rc", None)], [("rp", None)]], [("a0", hw * i, hw * i + hw, [first], off[p], ("a0", "a0"))])
+    for m in range(MB):
+        p, lo, hi = ports[m % 2], NC * m, NC * m + NC
+        rc, rp, sem = "rc%d" % m, "rp%d" % m, "in%d" % m
+        put(last, [[("q_px%d" % m, 1)]] * 2, [("a0", lo, hi, [p], on[last], (rc, rp))])
+        put(p, [[(rc, None)], [(rp, None)]], [("a0", lo, hi, [first], off[p], (sem, sem))])
 
     used = set()
     for j, c in enumerate(cores):
@@ -94,31 +89,20 @@ def plan(T, topo):
         if to:
             put(c, [[("q_pw", 1)]] * 2, [("pw", 0, G * NC, [cores[k] for k in to], on[c], ("pwin", "pwin"))])
 
-    sem_of = {}
     for j, c in enumerate(cores):
         jobs = [w for w in ORDER[j] if isinstance(w, tuple)]
-        slot = {w: k for k, w in enumerate(jobs)}
-        leave = [(m, s) for m, s in jobs if s < n - 1 and HOST[m][s + 1] != j]
-        for group in LEAVE.get(j, [[(m,)] for m, s in leave]):
-            waits, moves = [], []
-            for i, run in enumerate(group):
-                outs = [v for m in run for v in leave if v[0] == m]
-                waits += [("q_%d" % slot[v], 1) for v in outs]
-                to = HOST[run[0]][outs[0][1] + 1]
-                d, buf, sem = cores[to], "a%d" % (outs[0][1] + 1), "in%d" % run[0]
-                lo, hi = NC * run[0], NC * run[-1] + NC
-                parts = {1: 1, 2: 2}.get(len(group), 4)
-                for m in run:
-                    sem_of[to, m] = sem
-                if topo.may_write(c, d):
-                    mask = on[c] if topo.chip(c) == topo.chip(d) else off[c]
-                    moves.append((buf, lo, hi, [d], share(mask, parts, i), (sem, sem)))
-                else:
-                    p = helpers(c, topo.die(c))[0]
-                    moves.append((buf, lo, hi, [p], share(on[c], parts, i), ("tc", "tp")))
-                    put(p, [[("tc", None)], [("tp", None)]], [(buf, lo, hi, [d], off[p], (sem, sem))])
-            put(c, [waits, waits], moves)
-    return calls, need, sem_of
+        for slot, (m, s) in enumerate(jobs):
+            if s == n - 1 or HOST[m][s + 1] == j:
+                continue
+            d, buf, sem, lo, hi = cores[HOST[m][s + 1]], "a%d" % (s + 1), "in%d" % m, NC * m, NC * m + NC
+            waits = [[("q_%d" % slot, 1)]] * 2
+            if topo.may_write(c, d):
+                put(c, waits, [(buf, lo, hi, [d], on[c] if topo.chip(c) == topo.chip(d) else off[c], (sem, sem))])
+            else:
+                p = helpers(c, topo.die(c))[0]
+                put(c, waits, [(buf, lo, hi, [p], on[c], ("tc", "tp"))])
+                put(p, [[("tc", None)], [("tp", None)]], [(buf, lo, hi, [d], off[p], (sem, sem))])
+    return calls, need
 
 
 def half(buf, part):
@@ -126,10 +110,10 @@ def half(buf, part):
 
 
 def rank_program(g, core, T, topo):
-    calls, need, sem_of = plan(T, topo)
+    calls, need = plan(T, topo)
     rank = T.rank_of(core)
     if rank is not None:
-        compute(g, rank, T, topo, need[core], sem_of)
+        compute(g, rank, T, topo, need[core])
     sent = 0
     for waits, part, moves in calls[core]:
         for name, val in waits:
@@ -155,7 +139,7 @@ def rank_program(g, core, T, topo):
         g.wait_ge(T.sem.sent, sent)
 
 
-def compute(g, rank, T, topo, need, sem_of):
+def compute(g, rank, T, topo, need):
     n = len(T.cores)
     S = T.sem
     last = rank == n - 1
@@ -170,20 +154,20 @@ def compute(g, rank, T, topo, need, sem_of):
             seen.add((qn, name, v))
             q.wait_ge(S[name], v)
 
-    hw = 4 * MB * NC // 2
     if last:
-        sy.dma_start(T.pxb[:, 0:hw], T.px[:, 0:hw]).then_inc(S.ld_px0, 16)
-        ac.dma_start(T.pxb[:, hw:2 * hw], T.px[:, hw:2 * hw]).then_inc(S.ld_px1, 16)
+        for m in range(MB):
+            lo, hi = 4 * NC * m, 4 * NC * m + 4 * NC
+            (ac if m % 2 else sy).dma_start(T.pxb[:, lo:hi], T.px[:, lo:hi]).then_inc(S["ld_px%d" % m], 16)
     sy.dma_start(T.xb[:], T.x[:]).then_inc(S.ld_x, 16)
     ac.dma_start(T.w1b[:], T.w1[:]).then_inc(S.ld_w1, 16)
     sy.dma_start(T.pwb[:], T.pw[:]).then_inc(S.ld_pw, 16)
     ac.dma_start(T.w2b[:], T.w2[:]).then_inc(S.ld_w2, 16)
 
     if last:
-        for i in range(2):
-            wait(ve, "v", "ld_px%d" % i, 16)
-            lo, hi = hw // 4 * i, hw // 4 * (i + 1)
-            ve.quantize_mx(T.a0q[:, lo:hi], T.a0s[:, lo:hi], T.pxb[:, 4 * lo:4 * hi]).then_inc(S.q_px, 1)
+        for m in range(MB):
+            wait(ve, "v", "ld_px%d" % m, 16)
+            lo, hi = NC * m, NC * m + NC
+            ve.quantize_mx(T.a0q[:, lo:hi], T.a0s[:, lo:hi], T.pxb[:, 4 * lo:4 * hi]).then_inc(S["q_px%d" % m], 1)
     wait(ve, "v", "ld_x", 16)
     ve.quantize_mx(T.xq[:, 0:128], T.xs[:, 0:128], T.xb[:, 0:512]).then_inc(S.q_xw, 1)
     wait(ve, "v", "ld_w1", 16)
@@ -249,7 +233,7 @@ def compute(g, rank, T, topo, need, sem_of):
             if s > 0 and HOST[m][s - 1] == rank:
                 wait(te, "t", "q_%d" % where[m], 1)
             else:
-                wait(te, "t", sem_of[rank, m] if s else "a0")
+                wait(te, "t", "in%d" % m)
             if s == rank:
                 wait(te, "t", "q_pw", 1)
                 w, ws = T.pwq, T.pws

@@ -6,16 +6,20 @@ G = 2
 MB = 3
 SIM = 16
 C = 0.031
+CODES, PLANES = 0, 1
 
-HOST = [[0, 1, 1, 3, 4, 5],
-        [0, 2, 1, 3, 3, 5],
-        [0, 2, 2, 4, 4, 5]]
+HOST = [[0, 2, 1, 4, 4, 5],
+        [0, 1, 1, 3, 4, 5],
+        [0, 2, 2, 3, 3, 5]]
 ORDER = [["h", (0, 0), (1, 0), (2, 0), "near", "far"],
-         ["h", (0, 1), (0, 2), "near", (1, 2), "far"],
-         ["h", (1, 1), (2, 1), (2, 2), "near", "far"],
-         ["h", "near", (0, 3), "far", (1, 3), (1, 4)],
-         ["h", "near", "far", (0, 4), (2, 3), (2, 4)],
+         ["h", (1, 1), (1, 2), (0, 2), "near", "far"],
+         ["h", (0, 1), (2, 1), (2, 2), "near", "far"],
+         ["h", "near", (1, 3), (2, 3), (2, 4), "far"],
+         ["h", "near", (0, 3), (0, 4), (1, 4), "far"],
          ["h", "near", "far", (0, 5), (1, 5), (2, 5)]]
+ENTRY = [(0, PLANES), (1, PLANES), (0, CODES), (1, CODES), (2, PLANES), (2, CODES)]
+ENTRY_PORT = [0, 2, 0]
+H_PORT = [0, None, 0, 0, 1, 1]
 
 BF, CODE, U8, F32 = "bfloat16", "float8_e4m3fn_x4", "uint8", "float32"
 SCRATCH = {
@@ -29,10 +33,10 @@ for _n, _w in [("x", 128), ("w1", 256), ("w2", 128), ("pw", 256), ("pr", 256), (
     SCRATCH[_n + "q"] = ("sbuf", [128, _w], CODE)
     SCRATCH[_n + "s"] = ("sbuf", [128, _w], U8)
 SEMAPHORES = (["ld_x", "ld_w1", "ld_w2", "ld_pw", "q_xw", "q_pw", "q_w2",
-               "mm_h0", "mm_h1", "ac_h", "ve_h", "q_h", "mm_near", "mm_far", "cp_near", "cp_far", "st"]
+               "mm0_h", "mm1_h", "ac_h", "ve_h", "q_h", "mm_near", "mm_far", "cp_near", "cp_far", "st"]
               + ["%s_%d" % (n, k) for k in range(3) for n in ("mm0", "mm1", "ac", "ve", "q")]
-              + ["%s%d" % (n, m) for m in range(MB) for n in ("ld_px", "q_px", "rc", "rp", "in")]
-              + ["nc", "np", "far", "pwin", "tc", "tp", "sent"])
+              + ["%s%d" % (n, m) for m in range(MB) for n in ("ld_px", "q_px", "out", "rc", "rp", "in")]
+              + ["nc", "np", "far", "pwin", "sent"])
 
 
 def bits(mask):
@@ -51,62 +55,66 @@ def plan(T, topo):
     def far(c):
         return [d for d in cores if topo.chip(d) != topo.chip(c)]
 
-    def helpers(c, die):
-        return [k for k in range(SIM) if k not in cores and topo.chip(k) == topo.chip(c) and topo.die(k) == die
-                and topo.may_write(k, far(c)[0])]
+    def helpers(c):
+        ks = [k for k in range(SIM) if k not in cores and topo.chip(k) == topo.chip(c) and topo.may_write(k, far(c)[0])]
+        return [k for k in ks if topo.die(k) == topo.die(c)] + [k for k in ks if topo.die(k) != topo.die(c)]
 
-    def put(src, waits, moves):
-        for part in range(2):
-            calls[src].append((waits[part], part, moves))
-            for buf, lo, hi, dsts, mask, sems in moves:
-                for d in dsts:
-                    need[d][sems[part]] = need[d].get(sems[part], 0) + len(bits(mask))
+    def put(src, part, waits, moves, local="sent"):
+        calls[src].append((waits, part, moves, local))
+        for buf, lo, hi, dsts, mask, sem in moves:
+            need[src][local] = need[src].get(local, 0) + len(bits(mask))
+            for d in dsts:
+                need[d][sem] = need[d].get(sem, 0) + len(bits(mask))
 
     on = {c: topo.mask(c, [d for d in range(SIM) if d != c and topo.chip(d) == topo.chip(c)][0]) for c in range(SIM)}
     off = {c: topo.mask(c, [d for d in range(SIM) if topo.chip(d) != topo.chip(c)][0]) for c in range(SIM)}
     last, first = cores[n - 1], cores[0]
 
-    ports = [helpers(last, topo.die(last))[0], helpers(last, 1 - topo.die(last))[0]]
-    for m in range(MB):
-        p, lo, hi = ports[m % 2], NC * m, NC * m + NC
-        rc, rp, sem = "rc%d" % m, "rp%d" % m, "in%d" % m
-        put(last, [[("q_px%d" % m, 1)]] * 2, [("a0", lo, hi, [p], on[last], (rc, rp))])
-        put(p, [[(rc, None)], [(rp, None)]], [("a0", lo, hi, [first], off[p], (sem, sem))])
+    for m, part in ENTRY:
+        p, lo, hi = helpers(last)[ENTRY_PORT[m]], NC * m, NC * m + NC
+        via = ("rp%d" if part == PLANES else "rc%d") % m
+        put(last, part, [("q_px%d" % m, 1)], [("a0", lo, hi, [p], off[last] if part == PLANES else on[last], via)], "out%d" % m)
+        put(p, part, [(via, None)], [("a0", lo, hi, [first], off[p], "in%d" % m)])
 
-    used = set()
     for j, c in enumerate(cores):
         lo, hi = NC * j, NC * j + NC
-        if topo.may_write(c, far(c)[0]) and topo.chip(c) == topo.chip(first):
-            put(c, [[("q_h", 1)]] * 2, [("h", lo, hi, near(c), on[c] & ~off[c], ("nc", "np")), ("h", lo, hi, far(c), off[c], ("far", "far"))])
-        else:
-            p = [k for k in helpers(c, topo.die(c)) + helpers(c, 1 - topo.die(c)) if k not in used][0]
-            used.add(p)
-            put(c, [[("q_h", 1)]] * 2, [("h", lo, hi, near(c) + [p], on[c], ("nc", "np"))])
-            put(p, [[("nc", None)], [("np", None)]], [("h", lo, hi, far(c), off[p], ("far", "far"))])
+        for part in (CODES, PLANES):
+            sem = "nc" if part == CODES else "np"
+            if H_PORT[j] is None:
+                put(c, part, [("q_h", 1)], [("h", lo, hi, near(c), on[c] & ~off[c], sem), ("h", lo, hi, far(c), off[c], "far")])
+            else:
+                p = helpers(c)[H_PORT[j]]
+                put(c, part, [("q_h", 1)], [("h", lo, hi, near(c) + [p], on[c], sem)])
+                put(p, part, [(sem, None)], [("h", lo, hi, far(c), off[p], "far")])
 
     for j, c in enumerate(cores):
         to = sorted({HOST[m][j] for m in range(MB)} - {j})
         if to:
-            put(c, [[("q_pw", 1)]] * 2, [("pw", 0, G * NC, [cores[k] for k in to], on[c], ("pwin", "pwin"))])
+            for part in (CODES, PLANES):
+                put(c, part, [("q_pw", 1)], [("pw", 0, G * NC, [cores[k] for k in to], on[c], "pwin")])
 
     for j, c in enumerate(cores):
-        jobs = [w for w in ORDER[j] if isinstance(w, tuple)]
-        for slot, (m, s) in enumerate(jobs):
+        for slot, (m, s) in enumerate([w for w in ORDER[j] if isinstance(w, tuple)]):
             if s == n - 1 or HOST[m][s + 1] == j:
                 continue
-            d, buf, sem, lo, hi = cores[HOST[m][s + 1]], "a%d" % (s + 1), "in%d" % m, NC * m, NC * m + NC
-            waits = [[("q_%d" % slot, 1)]] * 2
+            d, buf, lo, hi = cores[HOST[m][s + 1]], "a%d" % (s + 1), NC * m, NC * m + NC
+            waits, sem = [("q_%d" % slot, 1)], "in%d" % m
             if topo.may_write(c, d):
-                put(c, waits, [(buf, lo, hi, [d], on[c] if topo.chip(c) == topo.chip(d) else off[c], (sem, sem))])
+                for part in (CODES, PLANES):
+                    put(c, part, waits, [(buf, lo, hi, [d], on[c] if topo.chip(c) == topo.chip(d) else off[c], sem)])
             else:
-                p = helpers(c, topo.die(c))[0]
-                put(c, waits, [(buf, lo, hi, [p], on[c], ("tc", "tp"))])
-                put(p, [[("tc", None)], [("tp", None)]], [(buf, lo, hi, [d], off[p], (sem, sem))])
+                p, o = helpers(c)[0], helpers(c)[-1]
+                mid = (lo + hi) // 2
+                put(c, PLANES, waits, [(buf, lo, hi, [p], on[c], "rp%d" % m)])
+                put(p, PLANES, [("rp%d" % m, None)], [(buf, lo, hi, [d], off[p], sem)])
+                put(c, CODES, waits, [(buf, lo, mid, [p], off[c], "rc%d" % m), (buf, mid, hi, [o], on[c] & ~off[c], "rc%d" % m)])
+                for k, a, b in ((p, lo, mid), (o, mid, hi)):
+                    put(k, CODES, [("rc%d" % m, None)], [(buf, a, b, [d], off[k], sem)])
     return calls, need
 
 
 def half(buf, part):
-    return buf + ("q" if part == 0 else "s")
+    return buf + ("q" if part == CODES else "s")
 
 
 def rank_program(g, core, T, topo):
@@ -114,29 +122,28 @@ def rank_program(g, core, T, topo):
     rank = T.rank_of(core)
     if rank is not None:
         compute(g, rank, T, topo, need[core])
-    sent = 0
-    for waits, part, moves in calls[core]:
+    for waits, part, moves, local in calls[core]:
         for name, val in waits:
             g.wait_ge(T.sem[name], need[core][name] if val is None else val)
         trs = []
-        for buf, lo, hi, dsts, mask, sems in moves:
+        for buf, lo, hi, dsts, mask, sem in moves:
             ap = T[half(buf, part)][:, lo:hi]
             out = T[half("pr" if buf == "pw" else buf, part)][:, lo:hi]
-            if part == 0:
+            if part == CODES:
                 ap, out = ap.bitcast(dt.uint8), out.bitcast(dt.uint8)
-            trs.append((ap, out, dsts, mask, T.sem[sems[part]]))
-            sent += len(bits(mask))
+            trs.append((ap, out, dsts, mask, T.sem[sem]))
         if len(trs) == 1 and len(trs[0][2]) == 1:
             ap, out, dsts, mask, sem = trs[0]
             rid, pid, _ = topo.addr(dsts[0])
-            g.remote_dma(out, ap, sem, T.sem.sent, pid, rid, mask)
+            g.remote_dma(out, ap, sem, T.sem[local], pid, rid, mask)
         else:
             g.remote_dma_fused([RemoteDMATransfer(
                 dst_ids=[DstId(rid=topo.addr(d)[0], pnc=topo.addr(d)[1]) for d in dsts],
                 dma_engine_mask=mask, remote_sem=sem, srcs=[ap], dsts=[out for d in dsts], alu_op=0)
-                for ap, out, dsts, mask, sem in trs], local_sem=T.sem.sent)
-    if sent:
-        g.wait_ge(T.sem.sent, sent)
+                for ap, out, dsts, mask, sem in trs], local_sem=T.sem[local])
+    for name in ["sent"] + ["out%d" % m for m in range(MB)]:
+        if name in need[core]:
+            g.wait_ge(T.sem[name], need[core][name])
 
 
 def compute(g, rank, T, topo, need):
@@ -158,6 +165,8 @@ def compute(g, rank, T, topo, need):
         for m in range(MB):
             lo, hi = 4 * NC * m, 4 * NC * m + 4 * NC
             (ac if m % 2 else sy).dma_start(T.pxb[:, lo:hi], T.px[:, lo:hi]).then_inc(S["ld_px%d" % m], 16)
+        wait(sy, "s", "out0")
+        wait(ac, "a", "out0")
     sy.dma_start(T.xb[:], T.x[:]).then_inc(S.ld_x, 16)
     ac.dma_start(T.w1b[:], T.w1[:]).then_inc(S.ld_w1, 16)
     sy.dma_start(T.pwb[:], T.pw[:]).then_inc(S.ld_pw, 16)
@@ -179,26 +188,23 @@ def compute(g, rank, T, topo, need):
         wait(ve, "v", "ld_w2", 16)
         ve.quantize_mx(T.w2q[:, 0:128], T.w2s[:, 0:128], T.w2b[:, 0:512]).then_inc(S.q_w2, 1)
 
-    def tag_mm(tag, i):
-        return "mm_h%d" % i if tag == "h" else "mm%d_%s" % (i, tag)
-
     def products(tag, bank, w, ws, q, s, lo):
         for i in range(G):
             te.matmul_mx(T.ps[:, 512 * (bank + i):512 * (bank + i) + NC], w[:, NC * i:NC * i + NC], ws[:, NC * i:NC * i + NC],
-                         q[:, lo:lo + NC], s[:, lo:lo + NC], True, True).then_inc(S[tag_mm(tag, i)], 1)
+                         q[:, lo:lo + NC], s[:, lo:lo + NC], True, True).then_inc(S["mm%d_%s" % (i, tag)], 1)
 
     def tile(tag, bank, tb, at, q, s, lo, sem):
         z0, z1 = T.ps[:, 512 * bank:512 * bank + NC], T.ps[:, 512 * bank + 512:512 * bank + 512 + NC]
-        a, v = S["ac_%s" % tag], S["ve_%s" % tag]
+        a, v = S["ac_" + tag], S["ve_" + tag]
         e = at + 4 * NC
-        wait(ac, "a", tag_mm(tag, 0), 1)
+        wait(ac, "a", "mm0_" + tag, 1)
         ac.activation(tb[:, at:e:4], z0, Relu, scale=C).then_inc(a, 1)
         ac.activation(tb[:, at + 1:e:4], z0, Relu, scale=-C).then_inc(a, 1)
-        wait(ve, "v", tag_mm(tag, 1), 1)
+        wait(ve, "v", "mm1_" + tag, 1)
         ve.tensor_scalar(tb[:, at + 2:e:4], z1, C, 0.0, mult, mx).then_inc(v, 1)
         ve.tensor_scalar(tb[:, at + 3:e:4], z1, -C, 0.0, mult, mx).then_inc(v, 1)
-        wait(ve, "v", "ve_%s" % tag, 2)
-        wait(ve, "v", "ac_%s" % tag, 2)
+        wait(ve, "v", "ve_" + tag, 2)
+        wait(ve, "v", "ac_" + tag, 2)
         ve.quantize_mx(q[:, lo:lo + NC], s[:, lo:lo + NC], tb[:, at:e]).then_inc(S[sem], 1)
 
     mine = [j for j in range(n) if topo.chip(T.cores[j]) == topo.chip(T.cores[rank])]
@@ -221,8 +227,12 @@ def compute(g, rank, T, topo, need):
                 wait(te, "t", name)
             z = T.ps[:, 512 * bank:512 * bank + hi - lo]
             te.matmul_mx(z, T.w2q[:, 0:NC], T.w2s[:, 0:NC], T.hq[:, lo:hi], T.hs[:, lo:hi], True, True).then_inc(S["mm_" + job], 1)
-            wait(ac, "a", "mm_" + job, 1)
-            ac.activation(T.yb[:, lo:hi], z, Copy).then_inc(S["cp_" + job], 1)
+            if job == "near":
+                wait(ac, "a", "mm_near", 1)
+                ac.activation(T.yb[:, lo:hi], z, Copy).then_inc(S.cp_near, 1)
+            else:
+                wait(ve, "v", "mm_far", 1)
+                ve.tensor_copy(T.yb[:, lo:hi], z).then_inc(S.cp_far, 1)
             wait(sy, "s", "cp_" + job, 1)
             sy.dma_start(T.y[:, lo:hi], T.yb[:, lo:hi]).then_inc(S.st, 16)
             stores += 1
@@ -249,10 +259,10 @@ def compute(g, rank, T, topo, need):
                 ac.activation(T.zb[:, lo:lo + NC], T.ps[:, 512 * bank:512 * bank + NC], Copy).then_inc(S["ac_" + tag], 1)
                 wait(ve, "v", "mm1_" + tag, 1)
                 ve.tensor_copy(T.zb[:, lo + NC:lo + 2 * NC], T.ps[:, 512 * bank + 512:512 * bank + 512 + NC]).then_inc(S["ve_" + tag], 1)
-                wait(sy, "s", "ac_" + tag, 1)
-                wait(sy, "s", "ve_" + tag, 1)
-                sy.dma_start(T.z[:, lo:lo + 2 * NC], T.zb[:, lo:lo + 2 * NC]).then_inc(S.st, 16)
-                stores += 1
+                for i, name in enumerate(("ac_", "ve_")):
+                    wait(sy, "s", name + tag, 1)
+                    sy.dma_start(T.z[:, lo + NC * i:lo + NC * i + NC], T.zb[:, lo + NC * i:lo + NC * i + NC]).then_inc(S.st, 16)
+                    stores += 1
             where[m] = slot
             slot += 1
     wait(sy, "s", "st", 16 * stores)

from concourse.bass import DstId, RemoteDMATransfer
from concourse.mybir import dt, AluOpType, ActivationFunctionType

NC = 128
G = 2
MB = 3
SIM = 16
C = 0.031
CODES, PLANES = 0, 1

HOST = [[0, 2, 1, 4, 4, 5],
        [0, 1, 1, 3, 4, 5],
        [0, 2, 2, 3, 3, 5]]
ORDER = [["h", (0, 0), (1, 0), (2, 0), "near", "far"],
         ["h", (1, 1), (1, 2), (0, 2), "near", "far"],
         ["h", (0, 1), (2, 1), (2, 2), "near", "far"],
         ["h", "near", (1, 3), (2, 3), (2, 4), "far"],
         ["h", "near", (0, 3), (0, 4), (1, 4), "far"],
         ["h", "near", "far", (0, 5), (1, 5), (2, 5)]]
ENTRY = [(0, PLANES), (1, PLANES), (0, CODES), (1, CODES), (2, PLANES), (2, CODES)]
ENTRY_PORT = [0, 2, 0]
H_PORT = [0, None, 0, 0, 1, 1]

BF, CODE, U8, F32 = "bfloat16", "float8_e4m3fn_x4", "uint8", "float32"
SCRATCH = {
    "xb": ("sbuf", [128, 512], BF), "w1b": ("sbuf", [128, 1024], BF), "w2b": ("sbuf", [128, 512], BF),
    "pwb": ("sbuf", [128, 1024], BF), "pxb": ("sbuf", [128, 1536], BF),
    "ht": ("sbuf", [128, 512], BF), "ct": ("sbuf", [128, 1536], BF),
    "yb": ("sbuf", [128, 768], F32), "zb": ("sbuf", [128, 768], F32),
    "ps": ("psum", [128, 4096], F32),
}
for _n, _w in [("x", 128), ("w1", 256), ("w2", 128), ("pw", 256), ("pr", 256), ("h", 768)] + [("a%d" % k, 384) for k in range(6)]:
    SCRATCH[_n + "q"] = ("sbuf", [128, _w], CODE)
    SCRATCH[_n + "s"] = ("sbuf", [128, _w], U8)
SEMAPHORES = (["ld_x", "ld_w1", "ld_w2", "ld_pw", "q_xw", "q_pw", "q_w2",
               "mm0_h", "mm1_h", "ac_h", "ve_h", "q_h", "mm_near", "mm_far", "cp_near", "cp_far", "st"]
              + ["%s_%d" % (n, k) for k in range(3) for n in ("mm0", "mm1", "ac", "ve", "q")]
              + ["%s%d" % (n, m) for m in range(MB) for n in ("ld_px", "q_px", "out", "rc", "rp", "in")]
              + ["nc", "np", "far", "pwin", "sent"])


def bits(mask):
    return [1 << b for b in range(16) if mask >> b & 1]


def plan(T, topo):
    cores = T.cores
    n = len(cores)
    calls = {c: [] for c in range(SIM)}
    need = {c: {} for c in range(SIM)}

    def near(c):
        return [d for d in cores if d != c and topo.chip(d) == topo.chip(c)]

    def far(c):
        return [d for d in cores if topo.chip(d) != topo.chip(c)]

    def helpers(c):
        ks = [k for k in range(SIM) if k not in cores and topo.chip(k) == topo.chip(c) and topo.may_write(k, far(c)[0])]
        return [k for k in ks if topo.die(k) == topo.die(c)] + [k for k in ks if topo.die(k) != topo.die(c)]

    def put(src, part, waits, moves, local="sent"):
        calls[src].append((waits, part, moves, local))
        for buf, lo, hi, dsts, mask, sem in moves:
            need[src][local] = need[src].get(local, 0) + len(bits(mask))
            for d in dsts:
                need[d][sem] = need[d].get(sem, 0) + len(bits(mask))

    on = {c: topo.mask(c, [d for d in range(SIM) if d != c and topo.chip(d) == topo.chip(c)][0]) for c in range(SIM)}
    off = {c: topo.mask(c, [d for d in range(SIM) if topo.chip(d) != topo.chip(c)][0]) for c in range(SIM)}
    last, first = cores[n - 1], cores[0]

    for m, part in ENTRY:
        p, lo, hi = helpers(last)[ENTRY_PORT[m]], NC * m, NC * m + NC
        via = ("rp%d" if part == PLANES else "rc%d") % m
        put(last, part, [("q_px%d" % m, 1)], [("a0", lo, hi, [p], off[last] if part == PLANES else on[last], via)], "out%d" % m)
        put(p, part, [(via, None)], [("a0", lo, hi, [first], off[p], "in%d" % m)])

    for j, c in enumerate(cores):
        lo, hi = NC * j, NC * j + NC
        for part in (CODES, PLANES):
            sem = "nc" if part == CODES else "np"
            if H_PORT[j] is None:
                put(c, part, [("q_h", 1)], [("h", lo, hi, near(c), on[c] & ~off[c], sem), ("h", lo, hi, far(c), off[c], "far")])
            else:
                p = helpers(c)[H_PORT[j]]
                put(c, part, [("q_h", 1)], [("h", lo, hi, near(c) + [p], on[c], sem)])
                put(p, part, [(sem, None)], [("h", lo, hi, far(c), off[p], "far")])

    for j, c in enumerate(cores):
        to = sorted({HOST[m][j] for m in range(MB)} - {j})
        if to:
            for part in (CODES, PLANES):
                put(c, part, [("q_pw", 1)], [("pw", 0, G * NC, [cores[k] for k in to], on[c], "pwin")])

    for j, c in enumerate(cores):
        for slot, (m, s) in enumerate([w for w in ORDER[j] if isinstance(w, tuple)]):
            if s == n - 1 or HOST[m][s + 1] == j:
                continue
            d, buf, lo, hi = cores[HOST[m][s + 1]], "a%d" % (s + 1), NC * m, NC * m + NC
            waits, sem = [("q_%d" % slot, 1)], "in%d" % m
            if topo.may_write(c, d):
                for part in (CODES, PLANES):
                    put(c, part, waits, [(buf, lo, hi, [d], on[c] if topo.chip(c) == topo.chip(d) else off[c], sem)])
            else:
                p, o = helpers(c)[0], helpers(c)[-1]
                mid = (lo + hi) // 2
                put(c, PLANES, waits, [(buf, lo, hi, [p], on[c], "rp%d" % m)])
                put(p, PLANES, [("rp%d" % m, None)], [(buf, lo, hi, [d], off[p], sem)])
                put(c, CODES, waits, [(buf, lo, mid, [p], off[c], "rc%d" % m), (buf, mid, hi, [o], on[c] & ~off[c], "rc%d" % m)])
                for k, a, b in ((p, lo, mid), (o, mid, hi)):
                    put(k, CODES, [("rc%d" % m, None)], [(buf, a, b, [d], off[k], sem)])
    return calls, need


def half(buf, part):
    return buf + ("q" if part == CODES else "s")


def rank_program(g, core, T, topo):
    calls, need = plan(T, topo)
    rank = T.rank_of(core)
    if rank is not None:
        compute(g, rank, T, topo, need[core])
    for waits, part, moves, local in calls[core]:
        for name, val in waits:
            g.wait_ge(T.sem[name], need[core][name] if val is None else val)
        trs = []
        for buf, lo, hi, dsts, mask, sem in moves:
            ap = T[half(buf, part)][:, lo:hi]
            out = T[half("pr" if buf == "pw" else buf, part)][:, lo:hi]
            if part == CODES:
                ap, out = ap.bitcast(dt.uint8), out.bitcast(dt.uint8)
            trs.append((ap, out, dsts, mask, T.sem[sem]))
        if len(trs) == 1 and len(trs[0][2]) == 1:
            ap, out, dsts, mask, sem = trs[0]
            rid, pid, _ = topo.addr(dsts[0])
            g.remote_dma(out, ap, sem, T.sem[local], pid, rid, mask)
        else:
            g.remote_dma_fused([RemoteDMATransfer(
                dst_ids=[DstId(rid=topo.addr(d)[0], pnc=topo.addr(d)[1]) for d in dsts],
                dma_engine_mask=mask, remote_sem=sem, srcs=[ap], dsts=[out for d in dsts], alu_op=0)
                for ap, out, dsts, mask, sem in trs], local_sem=T.sem[local])
    for name in ["sent"] + ["out%d" % m for m in range(MB)]:
        if name in need[core]:
            g.wait_ge(T.sem[name], need[core][name])


def compute(g, rank, T, topo, need):
    n = len(T.cores)
    S = T.sem
    last = rank == n - 1
    te, ve, ac, sy = g.tensor, g.vector, g.scalar, g.sync
    Relu, Copy = ActivationFunctionType.Relu, ActivationFunctionType.Copy
    mult, mx = AluOpType.mult, AluOpType.max
    seen = set()

    def wait(q, qn, name, val=None):
        v = need[name] if val is None else val
        if (qn, name, v) not in seen:
            seen.add((qn, name, v))
            q.wait_ge(S[name], v)

    if last:
        for m in range(MB):
            lo, hi = 4 * NC * m, 4 * NC * m + 4 * NC
            (ac if m % 2 else sy).dma_start(T.pxb[:, lo:hi], T.px[:, lo:hi]).then_inc(S["ld_px%d" % m], 16)
        wait(sy, "s", "out0")
        wait(ac, "a", "out0")
    sy.dma_start(T.xb[:], T.x[:]).then_inc(S.ld_x, 16)
    ac.dma_start(T.w1b[:], T.w1[:]).then_inc(S.ld_w1, 16)
    sy.dma_start(T.pwb[:], T.pw[:]).then_inc(S.ld_pw, 16)
    ac.dma_start(T.w2b[:], T.w2[:]).then_inc(S.ld_w2, 16)

    if last:
        for m in range(MB):
            wait(ve, "v", "ld_px%d" % m, 16)
            lo, hi = NC * m, NC * m + NC
            ve.quantize_mx(T.a0q[:, lo:hi], T.a0s[:, lo:hi], T.pxb[:, 4 * lo:4 * hi]).then_inc(S["q_px%d" % m], 1)
    wait(ve, "v", "ld_x", 16)
    ve.quantize_mx(T.xq[:, 0:128], T.xs[:, 0:128], T.xb[:, 0:512]).then_inc(S.q_xw, 1)
    wait(ve, "v", "ld_w1", 16)
    ve.quantize_mx(T.w1q[:, 0:256], T.w1s[:, 0:256], T.w1b[:, 0:1024]).then_inc(S.q_xw, 1)

    def late_inputs():
        wait(ve, "v", "ld_pw", 16)
        ve.quantize_mx(T.pwq[:, 0:256], T.pws[:, 0:256], T.pwb[:, 0:1024]).then_inc(S.q_pw, 1)
        wait(ve, "v", "ld_w2", 16)
        ve.quantize_mx(T.w2q[:, 0:128], T.w2s[:, 0:128], T.w2b[:, 0:512]).then_inc(S.q_w2, 1)

    def products(tag, bank, w, ws, q, s, lo):
        for i in range(G):
            te.matmul_mx(T.ps[:, 512 * (bank + i):512 * (bank + i) + NC], w[:, NC * i:NC * i + NC], ws[:, NC * i:NC * i + NC],
                         q[:, lo:lo + NC], s[:, lo:lo + NC], True, True).then_inc(S["mm%d_%s" % (i, tag)], 1)

    def tile(tag, bank, tb, at, q, s, lo, sem):
        z0, z1 = T.ps[:, 512 * bank:512 * bank + NC], T.ps[:, 512 * bank + 512:512 * bank + 512 + NC]
        a, v = S["ac_" + tag], S["ve_" + tag]
        e = at + 4 * NC
        wait(ac, "a", "mm0_" + tag, 1)
        ac.activation(tb[:, at:e:4], z0, Relu, scale=C).then_inc(a, 1)
        ac.activation(tb[:, at + 1:e:4], z0, Relu, scale=-C).then_inc(a, 1)
        wait(ve, "v", "mm1_" + tag, 1)
        ve.tensor_scalar(tb[:, at + 2:e:4], z1, C, 0.0, mult, mx).then_inc(v, 1)
        ve.tensor_scalar(tb[:, at + 3:e:4], z1, -C, 0.0, mult, mx).then_inc(v, 1)
        wait(ve, "v", "ve_" + tag, 2)
        wait(ve, "v", "ac_" + tag, 2)
        ve.quantize_mx(q[:, lo:lo + NC], s[:, lo:lo + NC], tb[:, at:e]).then_inc(S[sem], 1)

    mine = [j for j in range(n) if topo.chip(T.cores[j]) == topo.chip(T.cores[rank])]
    slot = 0
    where = {}
    stores = 0
    for job in ORDER[rank]:
        if job == "h":
            wait(te, "t", "q_xw", 2)
            products("h", 0, T.w1q, T.w1s, T.xq, T.xs, 0)
            tile("h", 0, T.ht, 0, T.hq, T.hs, NC * rank, "q_h")
            late_inputs()
        elif job in ("near", "far"):
            ranks = mine if job == "near" else [j for j in range(n) if j not in mine]
            lo, hi = NC * ranks[0], NC * ranks[-1] + NC
            bank = 0 if job == "near" else 1
            wait(te, "t", "q_w2", 1)
            wait(te, "t", "q_h", 1)
            for name in (("nc", "np") if job == "near" else ("far",)):
                wait(te, "t", name)
            z = T.ps[:, 512 * bank:512 * bank + hi - lo]
            te.matmul_mx(z, T.w2q[:, 0:NC], T.w2s[:, 0:NC], T.hq[:, lo:hi], T.hs[:, lo:hi], True, True).then_inc(S["mm_" + job], 1)
            if job == "near":
                wait(ac, "a", "mm_near", 1)
                ac.activation(T.yb[:, lo:hi], z, Copy).then_inc(S.cp_near, 1)
            else:
                wait(ve, "v", "mm_far", 1)
                ve.tensor_copy(T.yb[:, lo:hi], z).then_inc(S.cp_far, 1)
            wait(sy, "s", "cp_" + job, 1)
            sy.dma_start(T.y[:, lo:hi], T.yb[:, lo:hi]).then_inc(S.st, 16)
            stores += 1
        else:
            m, s = job
            bank = 2 + 2 * slot
            tag = str(slot)
            if s > 0 and HOST[m][s - 1] == rank:
                wait(te, "t", "q_%d" % where[m], 1)
            else:
                wait(te, "t", "in%d" % m)
            if s == rank:
                wait(te, "t", "q_pw", 1)
                w, ws = T.pwq, T.pws
            else:
                wait(te, "t", "pwin")
                w, ws = T.prq, T.prs
            products(tag, bank, w, ws, T["a%dq" % s], T["a%ds" % s], NC * m)
            if s < n - 1:
                tile(tag, bank, T.ct, 512 * slot, T["a%dq" % (s + 1)], T["a%ds" % (s + 1)], NC * m, "q_%d" % slot)
            else:
                lo = G * NC * m
                wait(ac, "a", "mm0_" + tag, 1)
                ac.activation(T.zb[:, lo:lo + NC], T.ps[:, 512 * bank:512 * bank + NC], Copy).then_inc(S["ac_" + tag], 1)
                wait(ve, "v", "mm1_" + tag, 1)
                ve.tensor_copy(T.zb[:, lo + NC:lo + 2 * NC], T.ps[:, 512 * bank + 512:512 * bank + 512 + NC]).then_inc(S["ve_" + tag], 1)
                for i, name in enumerate(("ac_", "ve_")):
                    wait(sy, "s", name + tag, 1)
                    sy.dma_start(T.z[:, lo + NC * i:lo + NC * i + NC], T.zb[:, lo + NC * i:lo + NC * i + NC]).then_inc(S.st, 16)
                    stores += 1
            where[m] = slot
            slot += 1
    wait(sy, "s", "st", 16 * stores)
